import numpy as np
import ml_dtypes


def mxq(x, axis, fmt="e4m3"):
    dtype, down = {"e4m3": (ml_dtypes.float8_e4m3fn, 7), "e5m2": (ml_dtypes.float8_e5m2, 14)}[fmt]
    v = np.moveaxis(np.asarray(x, np.float32).astype(ml_dtypes.bfloat16).astype(np.float64), axis, -1)
    blocks = v.reshape(v.shape[:-1] + (-1, 32))
    amax = np.abs(blocks).max(-1, keepdims=True)
    byte = np.maximum(np.where(amax > 0, np.frexp(amax)[1] - 1 + 127, 0) - down, 1)
    scale = np.exp2(byte - 127.0)
    codes = (blocks / scale).astype(np.float32).astype(dtype).astype(np.float64)
    return np.moveaxis((codes * scale).reshape(v.shape), -1, axis)


WIDE = False


def mx_kscale(k):
    if not WIDE:
        return np.ones(k)
    levels = np.array([10, -10, 5, -5, 0])
    if k % 512:
        return np.exp2(np.random.permutation(np.resize(levels, k // 32))).repeat(32)
    a = np.empty((k // 512, 16))
    for p in range(k // 512):
        a[p, :8] = np.random.permutation(np.resize(levels, 8))
        for g in range(8):
            far = levels[np.abs(levels - a[p, g]) >= 10]
            a[p, g + 8] = far[np.random.randint(len(far))]
    return np.exp2(a.ravel()).repeat(32)


def f64(x):
    return np.asarray(x).astype(np.float64)


def striped(idx):
    return np.tile(idx.reshape(-1, 16).T, (8, 1)).astype(np.uint16)


def unstriped(offs):
    return offs[:16].T.reshape(-1).astype(np.int64)


def striped8(idx):
    return np.concatenate([x.reshape(-1, 16).T for x in idx]).astype(np.uint16)


def runs(offs, k):
    lists = np.stack([offs[16 * r : 16 * r + 16].T.reshape(-1) for r in range(8)]).astype(np.int64)
    return lists[np.arange(k) % 512 // 64]


def pack_weight(w):
    k, n = w.shape
    w = f64(np.asarray(w, np.float32).astype(ml_dtypes.bfloat16)).reshape(k // 32, 32, n)
    amax = np.abs(w).max(1)
    byte = np.clip(np.where(amax > 0, np.frexp(amax)[1] - 1 + 127 - 7, 1), 1, 254)
    scaled = (w * np.exp2(127.0 - byte)[:, None, :]).reshape(k, n).astype(np.float32)
    words = np.ascontiguousarray(scaled.reshape(k // 512, 128, 4, n).transpose(0, 1, 3, 2)).astype(ml_dtypes.float8_e4m3fn).view(np.uint8)
    return words, np.ascontiguousarray(byte.astype(np.uint8).reshape(k // 512, 16, n))


def unpack_weight(words, scales):
    g, p, n, _ = words.shape
    vals = np.ascontiguousarray(words).view(ml_dtypes.float8_e4m3fn).astype(np.float64) * np.repeat(np.exp2(scales.astype(np.float64) - 127.0), 8, axis=1)[..., None]
    return vals.transpose(0, 1, 3, 2).reshape(g * 512, n)


def sigmoid(v):
    return 1.0 / (1.0 + np.exp(-np.maximum(v, -700.0)))


K, T, S, G, H, U = 512, 1024, 256, 2048, 512, 512


def setup_inputs():
    n = np.random.standard_normal
    s = mx_kscale(K)[:, None]
    packed_xT = pack_weight(n((K, T)) * s)
    packed_dT = pack_weight(n((K, G)) / s)
    perm = np.random.permutation(U)
    return {
        "x_words": packed_xT[0],
        "x_scales": packed_xT[1],
        "d_words": packed_dT[0],
        "d_scales": packed_dT[1],
        "sl": np.random.uniform(1.0, 2.0, (H, 1)).astype(np.float32),
        "th": (0.5 * n((H, 1))).astype(np.float32),
        "gs": (np.random.uniform(0.5, 1.5, (K, 1)) * s).astype(np.float32),
        "offs": striped8(np.random.randint(0, T, (8, S))),
        "ka": striped8(np.random.randint(0, G, (8, H))),
        "kb": striped8(np.random.randint(0, G, (8, H))),
        "n1": striped(np.random.permutation(S)),
        "n2": striped(np.random.permutation(S)),
        "k1": striped8(np.random.randint(0, G, (8, H))),
        "k2": striped8(np.random.randint(0, G, (8, H))),
        "two": striped(np.random.permutation(T)[:S]),
        "k3": striped8(np.random.randint(0, G, (8, H))),
        "hz": striped8(np.random.randint(0, T, (8, S))),
        "n3": striped(perm[:S]),
        "n4": striped(perm[S:]),
        "n5": striped(np.random.permutation(S)),
    }


def reference(x_words, x_scales, d_words, d_scales, sl, th, gs, offs, ka, kb, n1, n2, k1, k2, two, k3, hz, n3, n4, n5):
    d_k1 = unpack_weight(d_words, d_scales)[np.arange(K)[:, None], runs(k1, K)]
    d_ka = unpack_weight(d_words, d_scales)[np.arange(K)[:, None], runs(ka, K)]
    xq = unpack_weight(x_words, x_scales)[np.arange(K)[:, None], runs(offs, K)]
    d_kb = unpack_weight(d_words, d_scales)[np.arange(K)[:, None], runs(kb, K)]
    h = 0.0625 * (d_ka.T @ xq + d_kb.T @ xq)
    ds = np.zeros((H, S))
    ds[:, unstriped(n1)] = h
    sg = sigmoid(f64(sl) * (h[:, unstriped(n2)] - f64(th)))
    z = f64(gs) * (ds * sg)
    d_k2 = unpack_weight(d_words, d_scales)[np.arange(K)[:, None], runs(k2, K)]
    x_two = unpack_weight(x_words, x_scales)[:, unstriped(two)]
    d_k3 = unpack_weight(d_words, d_scales)[np.arange(K)[:, None], runs(k3, K)]
    x_hz = unpack_weight(x_words, x_scales)[np.arange(K)[:, None], runs(hz, K)]
    h2 = 0.0625 * ((d_k1.T @ mxq(z, 0, "e4m3") + d_k2.T @ x_two + d_k3.T @ x_hz))
    ds2 = np.zeros((H, S))
    ds2[:, unstriped(n5)] = h2
    up = np.maximum(h2, ds2)
    ph = np.zeros((H, U))
    ph[:, unstriped(n3)] = ds2
    out = ph.copy()
    out[:, unstriped(n4)] = up
    return out

@@ -1,0 +1,229 @@
+from contextlib import ExitStack
+
+import concourse.mybir as mybir
+
+K, T, S, G, H, U = 512, 1024, 256, 2048, 512, 512
+FLOPS = 2 * K * H * S * 5
+
+F32 = mybir.dt.float32
+BF16 = mybir.dt.bfloat16
+I32 = mybir.dt.int32
+U32 = mybir.dt.uint32
+U16 = mybir.dt.uint16
+U8 = mybir.dt.uint8
+FP8X4 = mybir.dt.float8_e4m3fn_x4
+ACT = mybir.ActivationFunctionType
+ALU = mybir.AluOpType
+
+P = 128
+PACK = 4
+HALF = S // 2
+WIDE = 384
+SIXTEENTH = 0.0625
+
+
+def tile_picked_ahzmthesndpagsn_none_p_kernel(
+    tc, x_words, x_scales, d_words, d_scales, sl, th, gs, offs, ka, kb, n1, n2, k1, k2, two, k3, hz, n3, n4, n5, out
+):
+    nc = tc.nc
+    with ExitStack() as ctx:
+        keep = ctx.enter_context(tc.tile_pool(name="keep", bufs=1))
+        psum = ctx.enter_context(tc.psum_pool(name="psum", bufs=1))
+
+        lists = {}
+
+        def load_list(name, src):
+            lists[name] = keep.tile(list(src.shape), U16, name="list_" + name)
+            nc.sync.dma_start(lists[name][:], src)
+
+        def entries(name, start, count):
+            return lists[name][:, start // 16 : (start + count) // 16]
+
+        d_bytes = keep.tile([P, G], U8, align_bytes=64)
+        x_bytes = keep.tile([P, T], U8, align_bytes=64)
+        d_codes = keep.tile([P, G], U32, align_bytes=64)
+        x_codes = keep.tile([P, T], U32, align_bytes=64)
+        nc.vector.memset(d_bytes[:].bitcast(I32), 0)
+        nc.gpsimd.memset(x_bytes[:].bitcast(I32), 0)
+        load_list("ka", ka)
+        load_list("kb", kb)
+        load_list("offs", offs)
+        nc.sync.dma_start(d_bytes[0:P:8, :].bitcast(I32), d_scales[0].bitcast(I32))
+        nc.sync.dma_start(x_bytes[0:P:8, :].bitcast(I32), x_scales[0].bitcast(I32))
+        nc.sync.dma_start(x_codes[:].bitcast(I32), x_words[0].rearrange("p n t -> p (n t)").bitcast(I32))
+        nc.sync.dma_start(d_codes[:].bitcast(I32), d_words[0].rearrange("p n t -> p (n t)").bitcast(I32))
+        rowwise = {}
+        for name, src in (("sl", sl), ("th", th), ("gs", gs)):
+            rowwise[name] = keep.tile([P, PACK], F32, name="row_" + name)
+            (nc.gpsimd if name == "gs" else nc.sync).dma_start(rowwise[name][:], src.rearrange("(p t) o -> p (t o)", t=PACK))
+        for name, src in (("n2", n2), ("n1", n1), ("k1", k1), ("k2", k2), ("k3", k3), ("two", two), ("hz", hz), ("n5", n5), ("n3", n3), ("n4", n4)):
+            load_list(name, src)
+
+        def zeroed_plane(name, width):
+            plane = keep.tile([P, width], U8, name=name, tag=name, align_bytes=64)
+            nc.vector.memset(plane[:].bitcast(I32), 0)
+            return plane
+
+        plane_a = zeroed_plane("plane_a", 2 * H + S)
+        plane_w = [zeroed_plane("plane_w%d" % b, 3 * S) for b in range(2)]
+        plane_x = zeroed_plane("plane_x", 2 * S)
+
+        def gather_bytes(picked, plane, picks, queues):
+            col = 0
+            for table, name, start, count in picks:
+                nc.vector.tensor_copy(picked[:, col : col + count], table[:].indirect(entries(name, start, count)))
+                col = col + count
+            for q in range(4):
+                queues[q % len(queues)].dma_start(plane[32 * q : 32 * q + 4, :].bitcast(I32), picked[32 * q : 32 * q + 32 : 8, :].bitcast(I32))
+
+        def gather_words(dst, table, name, start, count):
+            nc.vector.tensor_copy(dst, table[:].indirect(entries(name, start, count)))
+
+        def mx(acc, w_codes, w_plane, m_codes, m_plane, start, stop):
+            nc.tensor.matmul_mx(
+                out=acc, lhsT=w_codes.bitcast(FP8X4), lhsT_scale=w_plane, rhs=m_codes.bitcast(FP8X4), rhs_scale=m_plane, start=start, stop=stop
+            )
+
+        picked = keep.tile([P, 2 * H + S], U8, align_bytes=64)
+        gather_bytes(picked[:], plane_a, [(d_bytes, "ka", 0, H), (d_bytes, "kb", 0, H), (x_bytes, "offs", 0, S)], [nc.scalar])
+        xq = keep.tile([P, S], U32, align_bytes=64)
+        ab = keep.tile([P, 2 * H], U32, align_bytes=64)
+        gather_words(xq[:], x_codes, "offs", 0, S)
+        gather_words(ab[:, 0:H], d_codes, "ka", 0, H)
+        gather_words(ab[:, H : 2 * H], d_codes, "kb", 0, H)
+
+        bias = keep.tile([P, PACK], F32)
+        nc.vector.scalar_tensor_tensor(bias[:], rowwise["sl"][:], -1.0, rowwise["th"][:], ALU.mult, ALU.mult)
+
+        h = [keep.tile([P, S], F32, name="h%d" % t) for t in range(PACK)]
+        ds = [keep.tile([P, WIDE], F32, name="ds%d" % t) for t in range(PACK)]
+        sg = [keep.tile([P, S], F32, name="sg%d" % t) for t in range(PACK)]
+        z = [keep.tile([P, HALF, PACK], BF16, name="z%d" % a, align_bytes=64) for a in range(2)]
+        z_codes = [keep.tile([P, HALF], U32, name="z_codes%d" % a, align_bytes=64) for a in range(2)]
+        z_plane = [keep.tile([P, HALF], U8, name="z_plane%d" % a, align_bytes=64) for a in range(2)]
+        h_acc = []
+
+        def first_product(t):
+            codes = keep.tile([P, 2, P], U32, name="dealt_codes%d" % t, align_bytes=64)
+            plane = keep.tile([P, 2, P], U8, name="dealt_plane%d" % t, align_bytes=64)
+            nc.vector.tensor_copy(plane[:], plane_a[:, 0 : 2 * H].rearrange("p (w m t) -> p w m t", w=2, t=PACK)[:, :, :, t])
+            nc.vector.tensor_copy(codes[:], ab[:].rearrange("p (w m t) -> p w m t", w=2, t=PACK)[:, :, :, t])
+            acc = psum.tile([P, S], F32, name="h_acc%d" % t, tag="bank%d" % t)
+            for w in range(2):
+                mx(acc[:], codes[:, w, :], plane[:, w, :], xq[:], plane_a[:, 2 * H : 2 * H + S], w == 0, w == 1)
+            h_acc.append(acc)
+
+        def sigmoid_half(t, a):
+            nc.scalar.activation(
+                out=sg[t][:, a * HALF : (a + 1) * HALF],
+                in_=h[t][:].indirect(entries("n2", a * HALF, HALF)),
+                func=ACT.Sigmoid,
+                scale=rowwise["sl"][:, t : t + 1],
+                bias=bias[:, t : t + 1],
+            )
+
+        def first_step(t):
+            nc.vector.tensor_scalar(h[t][:], h_acc[t][:], SIXTEENTH, None, ALU.mult)
+            sigmoid_half(t, 0)
+            nc.scalar.activation(out=ds[t][:].indirect(entries("n1", 0, S)), in_=h[t][:], func=ACT.Copy)
+
+        def z_part(t, a):
+            cols = slice(a * HALF, (a + 1) * HALF)
+            nc.vector.scalar_tensor_tensor(z[a][:, :, t], ds[t][:, cols], rowwise["gs"][:, t : t + 1], sg[t][:, cols], ALU.mult, ALU.mult)
+
+        def quantise(a):
+            nc.vector.quantize_mx(out=z_codes[a][:].bitcast(FP8X4), scales=z_plane[a][:], in_=z[a][:].rearrange("p n t -> p (n t)"))
+
+        first_product(0)
+        for t in range(1, PACK):
+            first_product(t)
+            first_step(t - 1)
+        first_step(PACK - 1)
+
+        coded = ("k1", "k2", "k3")
+        gather_bytes(picked[:, 0 : 3 * S], plane_w[0], [(d_bytes, name, 0, S) for name in coded], [nc.sync])
+        gather_bytes(picked[:, 3 * S : 5 * S], plane_x, [(x_bytes, "two", 0, S), (x_bytes, "hz", 0, S)], [nc.sync])
+        x2 = [xq[:], ab[:, 3 * S : 4 * S]]
+        z_part(0, 0)
+        gather_words(x2[0], x_codes, "two", 0, S)
+        gather_words(x2[1], x_codes, "hz", 0, S)
+        z_part(1, 0)
+        gather_words(ab[:, S : 2 * S], d_codes, "k2", 0, S)
+        gather_words(ab[:, 2 * S : 3 * S], d_codes, "k3", 0, S)
+        gather_words(ab[:, 0:S], d_codes, "k1", 0, S)
+        z_part(2, 0)
+
+        h2 = [keep.tile([P, S], F32, name="h2_%d" % r) for r in range(4)]
+        ds2 = [keep.tile([P, WIDE], F32, name="ds2_%d" % r) for r in range(4)]
+        up = [keep.tile([P, S], F32, name="up%d" % r) for r in range(4)]
+        page = [keep.tile([P, U], F32, name="page%d" % r) for r in range(4)]
+
+        def open_group(acc, r, start, count):
+            for i in (1, 2):
+                rows = slice(i * S + (r % 2) * P, i * S + (r % 2 + 1) * P)
+                mx(
+                    acc,
+                    ab[:, rows],
+                    plane_w[r // 2][:, rows],
+                    x2[i - 1][:, start : start + count],
+                    plane_x[:, (i - 1) * S + start : (i - 1) * S + start + count],
+                    i == 1,
+                    False,
+                )
+
+        def z_pass(acc, r, a, stop):
+            rows = slice((r % 2) * P, (r % 2 + 1) * P)
+            mx(acc, ab[:, rows], plane_w[r // 2][:, rows], z_codes[a][:], z_plane[a][:], False, stop)
+
+        def send_n5(r, start, count):
+            nc.scalar.activation(out=ds2[r][:].indirect(entries("n5", start, count)), in_=h2[r][:, start : start + count], func=ACT.Copy)
+
+        def send_n3(r):
+            nc.vector.tensor_tensor(up[r][:], h2[r][:], ds2[r][:, 0:S], ALU.max)
+            nc.scalar.activation(out=page[r][:].indirect(entries("n3", 0, S)), in_=ds2[r][:, 0:S], func=ACT.Copy)
+
+        def send_n4(r):
+            nc.scalar.activation(out=page[r][:].indirect(entries("n4", 0, S)), in_=up[r][:], func=ACT.Copy)
+            nc.sync.dma_start(out[r * P : (r + 1) * P, :], page[r][:])
+
+        early = {}
+        for a in range(2):
+            for r in range(2):
+                early[r, a] = psum.tile([P, HALF], F32, name="early%d%d" % (r, a), tag="bank%d" % (4 + 2 * a + r))
+                open_group(early[r, a][:], r, a * HALF, HALF)
+
+        def close_early(a):
+            quantise(a)
+            for r in range(2):
+                z_pass(early[r, a][:], r, a, True)
+                nc.vector.tensor_scalar(h2[r][:, a * HALF : (a + 1) * HALF], early[r, a][:], SIXTEENTH, None, ALU.mult)
+                send_n5(r, a * HALF, HALF)
+
+        z_part(3, 0)
+        for t in range(PACK):
+            sigmoid_half(t, 1)
+        close_early(0)
+        for t in range(PACK):
+            z_part(t, 1)
+        close_early(1)
+
+        picked_late = keep.tile([P, 3 * S], U8, tag="plane_w0", align_bytes=64)
+        gather_bytes(picked_late[:], plane_w[1], [(d_bytes, name, S, S) for name in coded], [nc.sync])
+        send_n3(0)
+        send_n3(1)
+        for i, name in enumerate(coded):
+            gather_words(ab[:, i * S : (i + 1) * S], d_codes, name, S, S)
+        for r in (2, 3):
+            acc = psum.tile([P, S], F32, name="late%d" % r, tag="bank%d" % (r - 2))
+            open_group(acc[:], r, 0, S)
+            for a in range(2):
+                z_pass(acc[:, a * HALF : (a + 1) * HALF], r, a, a == 1)
+            nc.vector.tensor_scalar(h2[r][:], acc[:], SIXTEENTH, None, ALU.mult)
+        send_n4(0)
+        send_n5(2, 0, S)
+        send_n4(1)
+        send_n5(3, 0, S)
+        send_n3(2)
+        send_n3(3)
+        send_n4(2)
+        send_n4(3)

@@ -42,21 +42,25 @@ def tile_picked_ahzmthesndpagsn_none_p_kernel(
         d_bytes = keep.tile([P, G], U8, align_bytes=64)
         x_bytes = keep.tile([P, T], U8, align_bytes=64)
         d_codes = keep.tile([P, G], U32, align_bytes=64)
-        x_codes = keep.tile([P, T], U32, align_bytes=64)
+        x_codes = keep.tile([P, T], U32, tag="x_codes", align_bytes=64)
         nc.vector.memset(d_bytes[:].bitcast(I32), 0)
         nc.gpsimd.memset(x_bytes[:].bitcast(I32), 0)
+        warm = keep.tile([P, 2], F32)
+        nc.gpsimd.memset(warm[:, 0:1], 0.0)
+        nc.scalar.activation(out=warm[:, 1:2], in_=warm[:, 0:1], func=ACT.Sigmoid)
         load_list("ka", ka)
         load_list("kb", kb)
         load_list("offs", offs)
         nc.sync.dma_start(d_bytes[0:P:8, :].bitcast(I32), d_scales[0].bitcast(I32))
         nc.sync.dma_start(x_bytes[0:P:8, :].bitcast(I32), x_scales[0].bitcast(I32))
+        load_list("two", two)
         nc.sync.dma_start(x_codes[:].bitcast(I32), x_words[0].rearrange("p n t -> p (n t)").bitcast(I32))
         nc.sync.dma_start(d_codes[:].bitcast(I32), d_words[0].rearrange("p n t -> p (n t)").bitcast(I32))
         rowwise = {}
         for name, src in (("sl", sl), ("th", th), ("gs", gs)):
             rowwise[name] = keep.tile([P, PACK], F32, name="row_" + name)
-            (nc.gpsimd if name == "gs" else nc.sync).dma_start(rowwise[name][:], src.rearrange("(p t) o -> p (t o)", t=PACK))
-        for name, src in (("n2", n2), ("n1", n1), ("k1", k1), ("k2", k2), ("k3", k3), ("two", two), ("hz", hz), ("n5", n5), ("n3", n3), ("n4", n4)):
+            nc.gpsimd.dma_start(rowwise[name][:], src.rearrange("(p t) o -> p (t o)", t=PACK))
+        for name, src in (("hz", hz), ("k1", k1), ("k2", k2), ("k3", k3), ("n2", n2), ("n1", n1), ("n5", n5), ("n3", n3), ("n4", n4)):
             load_list(name, src)
 
         def zeroed_plane(name, width):
@@ -93,29 +97,40 @@ def tile_picked_ahzmthesndpagsn_none_p_kernel(
         gather_words(ab[:, H : 2 * H], d_codes, "kb", 0, H)
 
         bias = keep.tile([P, PACK], F32)
-        nc.vector.scalar_tensor_tensor(bias[:], rowwise["sl"][:], -1.0, rowwise["th"][:], ALU.mult, ALU.mult)
+        product = keep.tile([P, PACK], F32)
+        nc.gpsimd.tensor_tensor(product[:], rowwise["sl"][:], rowwise["th"][:], ALU.mult)
+        nc.gpsimd.tensor_scalar(bias[:], product[:], -1.0, 0.0, ALU.mult, ALU.add)
 
         h = [keep.tile([P, S], F32, name="h%d" % t) for t in range(PACK)]
-        ds = [keep.tile([P, WIDE], F32, name="ds%d" % t) for t in range(PACK)]
-        sg = [keep.tile([P, S], F32, name="sg%d" % t) for t in range(PACK)]
+        ds = [keep.tile([P, 2 * S], F32, name="ds%d" % t) for t in range(PACK)]
+        sg_first = keep.tile([P, HALF], F32)
+        sg = [sg_first[:], ds[0][:, S : S + HALF], ds[0][:, S + HALF : 2 * S], ds[1][:, S : S + HALF]]
         z = [keep.tile([P, HALF, PACK], BF16, name="z%d" % a, align_bytes=64) for a in range(2)]
+        z_rows = [keep.tile([P, PACK, HALF], BF16, name="z_rows%d" % a, tag=("x_codes", "z_rows1")[a], align_bytes=64) for a in range(2)]
         z_codes = [keep.tile([P, HALF], U32, name="z_codes%d" % a, align_bytes=64) for a in range(2)]
         z_plane = [keep.tile([P, HALF], U8, name="z_plane%d" % a, align_bytes=64) for a in range(2)]
         h_acc = []
+        dealt_codes = keep.tile([P, 2 * H], U32, align_bytes=64)
+        dealt_plane = keep.tile([P, 2 * H], U8, align_bytes=64)
+        nc.vector.tensor_copy(
+            dealt_codes[:].rearrange("p (t c i) -> p c t i", t=PACK, i=4), ab[:].rearrange("p (c i t) -> p c t i", t=PACK, i=4)
+        )
+        for planes in (slice(0, 1), slice(1, PACK)):
+            nc.vector.tensor_copy(
+                dealt_plane[:].rearrange("p (t c i) -> p c t i", t=PACK, i=16)[:, :, planes, :],
+                plane_a[:, 0 : 2 * H].rearrange("p (c i t) -> p c t i", t=PACK, i=16)[:, :, planes, :],
+            )
 
         def first_product(t):
-            codes = keep.tile([P, 2, P], U32, name="dealt_codes%d" % t, align_bytes=64)
-            plane = keep.tile([P, 2, P], U8, name="dealt_plane%d" % t, align_bytes=64)
-            nc.vector.tensor_copy(plane[:], plane_a[:, 0 : 2 * H].rearrange("p (w m t) -> p w m t", w=2, t=PACK)[:, :, :, t])
-            nc.vector.tensor_copy(codes[:], ab[:].rearrange("p (w m t) -> p w m t", w=2, t=PACK)[:, :, :, t])
             acc = psum.tile([P, S], F32, name="h_acc%d" % t, tag="bank%d" % t)
             for w in range(2):
-                mx(acc[:], codes[:, w, :], plane[:, w, :], xq[:], plane_a[:, 2 * H : 2 * H + S], w == 0, w == 1)
+                rows = slice((2 * t + w) * P, (2 * t + w + 1) * P)
+                mx(acc[:], dealt_codes[:, rows], dealt_plane[:, rows], xq[:], plane_a[:, 2 * H : 2 * H + S], w == 0, w == 1)
             h_acc.append(acc)
 
         def sigmoid_half(t, a):
             nc.scalar.activation(
-                out=sg[t][:, a * HALF : (a + 1) * HALF],
+                out=sg[t],
                 in_=h[t][:].indirect(entries("n2", a * HALF, HALF)),
                 func=ACT.Sigmoid,
                 scale=rowwise["sl"][:, t : t + 1],
@@ -123,13 +138,22 @@ def tile_picked_ahzmthesndpagsn_none_p_kernel(
             )
 
         def first_step(t):
-            nc.vector.tensor_scalar(h[t][:], h_acc[t][:], SIXTEENTH, None, ALU.mult)
+            if t == 0:
+                nc.scalar.activation(out=h[t][:], in_=h_acc[t][:], func=ACT.Copy, scale=SIXTEENTH)
+            else:
+                nc.vector.tensor_scalar(h[t][:], h_acc[t][:], SIXTEENTH, None, ALU.mult)
             sigmoid_half(t, 0)
             nc.scalar.activation(out=ds[t][:].indirect(entries("n1", 0, S)), in_=h[t][:], func=ACT.Copy)
 
         def z_part(t, a):
             cols = slice(a * HALF, (a + 1) * HALF)
-            nc.vector.scalar_tensor_tensor(z[a][:, :, t], ds[t][:, cols], rowwise["gs"][:, t : t + 1], sg[t][:, cols], ALU.mult, ALU.mult)
+            dst = z[0][:, :, t] if (t, a) == (PACK - 1, 0) else z_rows[a][:, t, :]
+            nc.vector.scalar_tensor_tensor(dst, ds[t][:, cols], rowwise["gs"][:, t : t + 1], sg[t], ALU.mult, ALU.mult)
+
+        def interleave(a, count):
+            nc.vector.tensor_copy(
+                z[a][:, :, 0:count].rearrange("p (c i) t -> p c t i", i=4), z_rows[a][:, 0:count, :].rearrange("p t (c i) -> p c t i", i=4)
+            )
 
         def quantise(a):
             nc.vector.quantize_mx(out=z_codes[a][:].bitcast(FP8X4), scales=z_plane[a][:], in_=z[a][:].rearrange("p n t -> p (n t)"))
@@ -141,39 +165,39 @@ def tile_picked_ahzmthesndpagsn_none_p_kernel(
         first_step(PACK - 1)
 
         coded = ("k1", "k2", "k3")
-        gather_bytes(picked[:, 0 : 3 * S], plane_w[0], [(d_bytes, name, 0, S) for name in coded], [nc.sync])
         gather_bytes(picked[:, 3 * S : 5 * S], plane_x, [(x_bytes, "two", 0, S), (x_bytes, "hz", 0, S)], [nc.sync])
-        x2 = [xq[:], ab[:, 3 * S : 4 * S]]
-        z_part(0, 0)
+        gather_bytes(picked[:, 0 : 3 * S], plane_w[0], [(d_bytes, name, 0, S) for name in coded], [nc.sync])
+        words = keep.tile([P, 5 * S], U32, tag="plane_a", align_bytes=64)
+        x2 = [words[:, 3 * S : 4 * S], words[:, 4 * S : 5 * S]]
         gather_words(x2[0], x_codes, "two", 0, S)
+        for i, name in enumerate(coded):
+            gather_words(words[:, i * S : (i + 1) * S], d_codes, name, 0, S)
         gather_words(x2[1], x_codes, "hz", 0, S)
-        z_part(1, 0)
-        gather_words(ab[:, S : 2 * S], d_codes, "k2", 0, S)
-        gather_words(ab[:, 2 * S : 3 * S], d_codes, "k3", 0, S)
-        gather_words(ab[:, 0:S], d_codes, "k1", 0, S)
-        z_part(2, 0)
+        for t in range(PACK - 1):
+            z_part(t, 0)
+        interleave(0, PACK - 1)
 
         h2 = [keep.tile([P, S], F32, name="h2_%d" % r) for r in range(4)]
         ds2 = [keep.tile([P, WIDE], F32, name="ds2_%d" % r) for r in range(4)]
         up = [keep.tile([P, S], F32, name="up%d" % r) for r in range(4)]
         page = [keep.tile([P, U], F32, name="page%d" % r) for r in range(4)]
 
-        def open_group(acc, r, start, count):
+        def x_passes(acc, r, start, count, first):
             for i in (1, 2):
                 rows = slice(i * S + (r % 2) * P, i * S + (r % 2 + 1) * P)
                 mx(
                     acc,
-                    ab[:, rows],
+                    words[:, rows],
                     plane_w[r // 2][:, rows],
                     x2[i - 1][:, start : start + count],
                     plane_x[:, (i - 1) * S + start : (i - 1) * S + start + count],
-                    i == 1,
-                    False,
+                    first and i == 1,
+                    not first and i == 2,
                 )
 
-        def z_pass(acc, r, a, stop):
+        def z_pass(acc, r, a, start, stop):
             rows = slice((r % 2) * P, (r % 2 + 1) * P)
-            mx(acc, ab[:, rows], plane_w[r // 2][:, rows], z_codes[a][:], z_plane[a][:], False, stop)
+            mx(acc, words[:, rows], plane_w[r // 2][:, rows], z_codes[a][:], z_plane[a][:], start, stop)
 
         def send_n5(r, start, count):
             nc.scalar.activation(out=ds2[r][:].indirect(entries("n5", start, count)), in_=h2[r][:, start : start + count], func=ACT.Copy)
@@ -190,13 +214,22 @@ def tile_picked_ahzmthesndpagsn_none_p_kernel(
         for a in range(2):
             for r in range(2):
                 early[r, a] = psum.tile([P, HALF], F32, name="early%d%d" % (r, a), tag="bank%d" % (4 + 2 * a + r))
-                open_group(early[r, a][:], r, a * HALF, HALF)
+                if (r, a) != (1, 1):
+                    x_passes(early[r, a][:], r, a * HALF, HALF, True)
 
         def close_early(a):
             quantise(a)
             for r in range(2):
-                z_pass(early[r, a][:], r, a, True)
-                nc.vector.tensor_scalar(h2[r][:, a * HALF : (a + 1) * HALF], early[r, a][:], SIXTEENTH, None, ALU.mult)
+                if (r, a) != (1, 1):
+                    z_pass(early[r, a][:], r, a, False, True)
+                else:
+                    z_pass(early[r, a][:], r, a, True, False)
+                    x_passes(early[r, a][:], r, a * HALF, HALF, False)
+                if a == 0:
+                    nc.scalar.activation(out=h2[r][:, 0:HALF], in_=early[r, a][:], func=ACT.Copy, scale=SIXTEENTH)
+                else:
+                    nc.vector.tensor_scalar(h2[r][:, HALF:S], early[r, a][:], SIXTEENTH, None, ALU.mult)
+            for r in range(2):
                 send_n5(r, a * HALF, HALF)
 
         z_part(3, 0)
@@ -205,6 +238,7 @@ def tile_picked_ahzmthesndpagsn_none_p_kernel(
         close_early(0)
         for t in range(PACK):
             z_part(t, 1)
+        interleave(1, PACK)
         close_early(1)
 
         picked_late = keep.tile([P, 3 * S], U8, tag="plane_w0", align_bytes=64)
@@ -212,12 +246,12 @@ def tile_picked_ahzmthesndpagsn_none_p_kernel(
         send_n3(0)
         send_n3(1)
         for i, name in enumerate(coded):
-            gather_words(ab[:, i * S : (i + 1) * S], d_codes, name, S, S)
+            gather_words(words[:, i * S : (i + 1) * S], d_codes, name, S, S)
         for r in (2, 3):
             acc = psum.tile([P, S], F32, name="late%d" % r, tag="bank%d" % (r - 2))
-            open_group(acc[:], r, 0, S)
+            x_passes(acc[:], r, 0, S, True)
             for a in range(2):
-                z_pass(acc[:, a * HALF : (a + 1) * HALF], r, a, a == 1)
+                z_pass(acc[:, a * HALF : (a + 1) * HALF], r, a, False, a == 1)
             nc.vector.tensor_scalar(h2[r][:], acc[:], SIXTEENTH, None, ALU.mult)
         send_n4(0)
         send_n5(2, 0, S)

from contextlib import ExitStack

import concourse.mybir as mybir

K, T, S, G, H, U = 512, 1024, 256, 2048, 512, 512
FLOPS = 2 * K * H * S * 5

F32 = mybir.dt.float32
BF16 = mybir.dt.bfloat16
I32 = mybir.dt.int32
U32 = mybir.dt.uint32
U16 = mybir.dt.uint16
U8 = mybir.dt.uint8
FP8X4 = mybir.dt.float8_e4m3fn_x4
ACT = mybir.ActivationFunctionType
ALU = mybir.AluOpType

P = 128
PACK = 4
HALF = S // 2
WIDE = 384
SIXTEENTH = 0.0625


def tile_picked_ahzmthesndpagsn_none_p_kernel(
    tc, x_words, x_scales, d_words, d_scales, sl, th, gs, offs, ka, kb, n1, n2, k1, k2, two, k3, hz, n3, n4, n5, out
):
    nc = tc.nc
    with ExitStack() as ctx:
        keep = ctx.enter_context(tc.tile_pool(name="keep", bufs=1))
        psum = ctx.enter_context(tc.psum_pool(name="psum", bufs=1))

        lists = {}

        def load_list(name, src):
            lists[name] = keep.tile(list(src.shape), U16, name="list_" + name)
            nc.sync.dma_start(lists[name][:], src)

        def entries(name, start, count):
            return lists[name][:, start // 16 : (start + count) // 16]

        d_bytes = keep.tile([P, G], U8, align_bytes=64)
        x_bytes = keep.tile([P, T], U8, align_bytes=64)
        d_codes = keep.tile([P, G], U32, align_bytes=64)
        x_codes = keep.tile([P, T], U32, tag="x_codes", align_bytes=64)
        nc.vector.memset(d_bytes[:].bitcast(I32), 0)
        nc.gpsimd.memset(x_bytes[:].bitcast(I32), 0)
        warm = keep.tile([P, 2], F32)
        nc.gpsimd.memset(warm[:, 0:1], 0.0)
        nc.scalar.activation(out=warm[:, 1:2], in_=warm[:, 0:1], func=ACT.Sigmoid)
        load_list("ka", ka)
        load_list("kb", kb)
        load_list("offs", offs)
        nc.sync.dma_start(d_bytes[0:P:8, :].bitcast(I32), d_scales[0].bitcast(I32))
        nc.sync.dma_start(x_bytes[0:P:8, :].bitcast(I32), x_scales[0].bitcast(I32))
        load_list("two", two)
        nc.sync.dma_start(x_codes[:].bitcast(I32), x_words[0].rearrange("p n t -> p (n t)").bitcast(I32))
        nc.sync.dma_start(d_codes[:].bitcast(I32), d_words[0].rearrange("p n t -> p (n t)").bitcast(I32))
        rowwise = {}
        for name, src in (("sl", sl), ("th", th), ("gs", gs)):
            rowwise[name] = keep.tile([P, PACK], F32, name="row_" + name)
            nc.gpsimd.dma_start(rowwise[name][:], src.rearrange("(p t) o -> p (t o)", t=PACK))
        for name, src in (("hz", hz), ("k1", k1), ("k2", k2), ("k3", k3), ("n2", n2), ("n1", n1), ("n5", n5), ("n3", n3), ("n4", n4)):
            load_list(name, src)

        def zeroed_plane(name, width):
            plane = keep.tile([P, width], U8, name=name, tag=name, align_bytes=64)
            nc.vector.memset(plane[:].bitcast(I32), 0)
            return plane

        plane_a = zeroed_plane("plane_a", 2 * H + S)
        plane_w = [zeroed_plane("plane_w%d" % b, 3 * S) for b in range(2)]
        plane_x = zeroed_plane("plane_x", 2 * S)

        def gather_bytes(picked, plane, picks, queues):
            col = 0
            for table, name, start, count in picks:
                nc.vector.tensor_copy(picked[:, col : col + count], table[:].indirect(entries(name, start, count)))
                col = col + count
            for q in range(4):
                queues[q % len(queues)].dma_start(plane[32 * q : 32 * q + 4, :].bitcast(I32), picked[32 * q : 32 * q + 32 : 8, :].bitcast(I32))

        def gather_words(dst, table, name, start, count):
            nc.vector.tensor_copy(dst, table[:].indirect(entries(name, start, count)))

        def mx(acc, w_codes, w_plane, m_codes, m_plane, start, stop):
            nc.tensor.matmul_mx(
                out=acc, lhsT=w_codes.bitcast(FP8X4), lhsT_scale=w_plane, rhs=m_codes.bitcast(FP8X4), rhs_scale=m_plane, start=start, stop=stop
            )

        picked = keep.tile([P, 2 * H + S], U8, align_bytes=64)
        gather_bytes(picked[:], plane_a, [(d_bytes, "ka", 0, H), (d_bytes, "kb", 0, H), (x_bytes, "offs", 0, S)], [nc.scalar])
        xq = keep.tile([P, S], U32, align_bytes=64)
        ab = keep.tile([P, 2 * H], U32, align_bytes=64)
        gather_words(xq[:], x_codes, "offs", 0, S)
        gather_words(ab[:, 0:H], d_codes, "ka", 0, H)
        gather_words(ab[:, H : 2 * H], d_codes, "kb", 0, H)

        bias = keep.tile([P, PACK], F32)
        product = keep.tile([P, PACK], F32)
        nc.gpsimd.tensor_tensor(product[:], rowwise["sl"][:], rowwise["th"][:], ALU.mult)
        nc.gpsimd.tensor_scalar(bias[:], product[:], -1.0, 0.0, ALU.mult, ALU.add)

        h = [keep.tile([P, S], F32, name="h%d" % t) for t in range(PACK)]
        ds = [keep.tile([P, 2 * S], F32, name="ds%d" % t) for t in range(PACK)]
        sg_first = keep.tile([P, HALF], F32)
        sg = [sg_first[:], ds[0][:, S : S + HALF], ds[0][:, S + HALF : 2 * S], ds[1][:, S : S + HALF]]
        z = [keep.tile([P, HALF, PACK], BF16, name="z%d" % a, align_bytes=64) for a in range(2)]
        z_rows = [keep.tile([P, PACK, HALF], BF16, name="z_rows%d" % a, tag=("x_codes", "z_rows1")[a], align_bytes=64) for a in range(2)]
        z_codes = [keep.tile([P, HALF], U32, name="z_codes%d" % a, align_bytes=64) for a in range(2)]
        z_plane = [keep.tile([P, HALF], U8, name="z_plane%d" % a, align_bytes=64) for a in range(2)]
        h_acc = []
        dealt_codes = keep.tile([P, 2 * H], U32, align_bytes=64)
        dealt_plane = keep.tile([P, 2 * H], U8, align_bytes=64)
        nc.vector.tensor_copy(
            dealt_codes[:].rearrange("p (t c i) -> p c t i", t=PACK, i=4), ab[:].rearrange("p (c i t) -> p c t i", t=PACK, i=4)
        )
        for planes in (slice(0, 1), slice(1, PACK)):
            nc.vector.tensor_copy(
                dealt_plane[:].rearrange("p (t c i) -> p c t i", t=PACK, i=16)[:, :, planes, :],
                plane_a[:, 0 : 2 * H].rearrange("p (c i t) -> p c t i", t=PACK, i=16)[:, :, planes, :],
            )

        def first_product(t):
            acc = psum.tile([P, S], F32, name="h_acc%d" % t, tag="bank%d" % t)
            for w in range(2):
                rows = slice((2 * t + w) * P, (2 * t + w + 1) * P)
                mx(acc[:], dealt_codes[:, rows], dealt_plane[:, rows], xq[:], plane_a[:, 2 * H : 2 * H + S], w == 0, w == 1)
            h_acc.append(acc)

        def sigmoid_half(t, a):
            nc.scalar.activation(
                out=sg[t],
                in_=h[t][:].indirect(entries("n2", a * HALF, HALF)),
                func=ACT.Sigmoid,
                scale=rowwise["sl"][:, t : t + 1],
                bias=bias[:, t : t + 1],
            )

        def first_step(t):
            if t == 0:
                nc.scalar.activation(out=h[t][:], in_=h_acc[t][:], func=ACT.Copy, scale=SIXTEENTH)
            else:
                nc.vector.tensor_scalar(h[t][:], h_acc[t][:], SIXTEENTH, None, ALU.mult)
            sigmoid_half(t, 0)
            nc.scalar.activation(out=ds[t][:].indirect(entries("n1", 0, S)), in_=h[t][:], func=ACT.Copy)

        def z_part(t, a):
            cols = slice(a * HALF, (a + 1) * HALF)
            dst = z[0][:, :, t] if (t, a) == (PACK - 1, 0) else z_rows[a][:, t, :]
            nc.vector.scalar_tensor_tensor(dst, ds[t][:, cols], rowwise["gs"][:, t : t + 1], sg[t], ALU.mult, ALU.mult)

        def interleave(a, count):
            nc.vector.tensor_copy(
                z[a][:, :, 0:count].rearrange("p (c i) t -> p c t i", i=4), z_rows[a][:, 0:count, :].rearrange("p t (c i) -> p c t i", i=4)
            )

        def quantise(a):
            nc.vector.quantize_mx(out=z_codes[a][:].bitcast(FP8X4), scales=z_plane[a][:], in_=z[a][:].rearrange("p n t -> p (n t)"))

        first_product(0)
        for t in range(1, PACK):
            first_product(t)
            first_step(t - 1)
        first_step(PACK - 1)

        coded = ("k1", "k2", "k3")
        gather_bytes(picked[:, 3 * S : 5 * S], plane_x, [(x_bytes, "two", 0, S), (x_bytes, "hz", 0, S)], [nc.sync])
        gather_bytes(picked[:, 0 : 3 * S], plane_w[0], [(d_bytes, name, 0, S) for name in coded], [nc.sync])
        words = keep.tile([P, 5 * S], U32, tag="plane_a", align_bytes=64)
        x2 = [words[:, 3 * S : 4 * S], words[:, 4 * S : 5 * S]]
        gather_words(x2[0], x_codes, "two", 0, S)
        for i, name in enumerate(coded):
            gather_words(words[:, i * S : (i + 1) * S], d_codes, name, 0, S)
        gather_words(x2[1], x_codes, "hz", 0, S)
        for t in range(PACK - 1):
            z_part(t, 0)
        interleave(0, PACK - 1)

        h2 = [keep.tile([P, S], F32, name="h2_%d" % r) for r in range(4)]
        ds2 = [keep.tile([P, WIDE], F32, name="ds2_%d" % r) for r in range(4)]
        up = [keep.tile([P, S], F32, name="up%d" % r) for r in range(4)]
        page = [keep.tile([P, U], F32, name="page%d" % r) for r in range(4)]

        def x_passes(acc, r, start, count, first):
            for i in (1, 2):
                rows = slice(i * S + (r % 2) * P, i * S + (r % 2 + 1) * P)
                mx(
                    acc,
                    words[:, rows],
                    plane_w[r // 2][:, rows],
                    x2[i - 1][:, start : start + count],
                    plane_x[:, (i - 1) * S + start : (i - 1) * S + start + count],
                    first and i == 1,
                    not first and i == 2,
                )

        def z_pass(acc, r, a, start, stop):
            rows = slice((r % 2) * P, (r % 2 + 1) * P)
            mx(acc, words[:, rows], plane_w[r // 2][:, rows], z_codes[a][:], z_plane[a][:], start, stop)

        def send_n5(r, start, count):
            nc.scalar.activation(out=ds2[r][:].indirect(entries("n5", start, count)), in_=h2[r][:, start : start + count], func=ACT.Copy)

        def send_n3(r):
            nc.vector.tensor_tensor(up[r][:], h2[r][:], ds2[r][:, 0:S], ALU.max)
            nc.scalar.activation(out=page[r][:].indirect(entries("n3", 0, S)), in_=ds2[r][:, 0:S], func=ACT.Copy)

        def send_n4(r):
            nc.scalar.activation(out=page[r][:].indirect(entries("n4", 0, S)), in_=up[r][:], func=ACT.Copy)
            nc.sync.dma_start(out[r * P : (r + 1) * P, :], page[r][:])

        early = {}
        for a in range(2):
            for r in range(2):
                early[r, a] = psum.tile([P, HALF], F32, name="early%d%d" % (r, a), tag="bank%d" % (4 + 2 * a + r))
                if (r, a) != (1, 1):
                    x_passes(early[r, a][:], r, a * HALF, HALF, True)

        def close_early(a):
            quantise(a)
            for r in range(2):
                if (r, a) != (1, 1):
                    z_pass(early[r, a][:], r, a, False, True)
                else:
                    z_pass(early[r, a][:], r, a, True, False)
                    x_passes(early[r, a][:], r, a * HALF, HALF, False)
                if a == 0:
                    nc.scalar.activation(out=h2[r][:, 0:HALF], in_=early[r, a][:], func=ACT.Copy, scale=SIXTEENTH)
                else:
                    nc.vector.tensor_scalar(h2[r][:, HALF:S], early[r, a][:], SIXTEENTH, None, ALU.mult)
            for r in range(2):
                send_n5(r, a * HALF, HALF)

        z_part(3, 0)
        for t in range(PACK):
            sigmoid_half(t, 1)
        close_early(0)
        for t in range(PACK):
            z_part(t, 1)
        interleave(1, PACK)
        close_early(1)

        picked_late = keep.tile([P, 3 * S], U8, tag="plane_w0", align_bytes=64)
        gather_bytes(picked_late[:], plane_w[1], [(d_bytes, name, S, S) for name in coded], [nc.sync])
        send_n3(0)
        send_n3(1)
        for i, name in enumerate(coded):
            gather_words(words[:, i * S : (i + 1) * S], d_codes, name, S, S)
        for r in (2, 3):
            acc = psum.tile([P, S], F32, name="late%d" % r, tag="bank%d" % (r - 2))
            x_passes(acc[:], r, 0, S, True)
            for a in range(2):
                z_pass(acc[:, a * HALF : (a + 1) * HALF], r, a, False, a == 1)
            nc.vector.tensor_scalar(h2[r][:], acc[:], SIXTEENTH, None, ALU.mult)
        send_n4(0)
        send_n5(2, 0, S)
        send_n4(1)
        send_n5(3, 0, S)
        send_n3(2)
        send_n3(3)
        send_n4(2)
        send_n4(3)
